import numpy as np, ml_dtypes
CORES = [17,57,65,89,97,121]
N = 6
CB = 2
def setup_inputs(rng):
    k = (rng.standard_normal((N, 128, CB * 128), dtype=np.float32) / 8).astype(ml_dtypes.bfloat16)
    kt = np.concatenate([k[:, :, 128 * c:128 * c + 128].transpose(0, 2, 1) for c in range(CB)], axis=2)
    tri = np.triu(np.ones((128, 128), np.float32)).astype(ml_dtypes.bfloat16)
    return {"q": (rng.standard_normal((N, 128, CB * 128), dtype=np.float32) / 8).astype(ml_dtypes.bfloat16), "k": k, "kt": kt, "v": rng.standard_normal((N, 128, CB * 128), dtype=np.float32).astype(ml_dtypes.bfloat16), "m": np.broadcast_to(tri, (N, 128, 128)).copy()}
def setup_inputs_big(rng):
    d = setup_inputs(rng)
    for k in ("q", "k", "kt", "v"): d[k] = (d[k].astype(np.float32) * 1024.0).astype(d[k].dtype)
    return d
def setup_inputs_small(rng):
    d = setup_inputs(rng)
    for k in ("q", "k", "kt", "v"): d[k] = (d[k].astype(np.float32) * (1 / 1024.0)).astype(d[k].dtype)
    return d
def setup_inputs_apart(rng):
    d = setup_inputs(rng)
    f = (10.0 ** rng.permutation(np.linspace(-1.5, 1.5, N))).astype(np.float32).reshape(N, 1, 1)
    for k in ("q", "k", "kt", "v"): d[k] = (d[k].astype(np.float32) * f).astype(d[k].dtype)
    return d
def reference(q, k, kt, v, m):
    Q, K, KT, V, M = q.astype(np.float64), k.astype(np.float64), kt.astype(np.float64), v.astype(np.float64), m.astype(np.float64)
    y = np.zeros((N, 128, CB * 128)); Z = np.zeros((128, 128))
    for r in range(N):
        for c in range(CB):
            s = slice(128 * c, 128 * c + 128)
            y[r][:, s] = Z.T @ Q[r][:, s] + V[r][:, s].T @ ((K[r][:, s].T @ Q[r][:, s]) * M[r])
            Z = Z + KT[r][:, s].T @ V[r][:, s]
    return {"y": y.astype(ml_dtypes.bfloat16)}

from concourse.bass import DstId, RemoteDMATransfer
from concourse.mybir import AluOpType

B = 128
W = 2 * B
N_RANKS = 6

SCRATCH = {
    "kt_sb": ("sbuf", [B, W], "bfloat16"),
    "v_sb": ("sbuf", [B, W], "bfloat16"),
    "k_sb": ("sbuf", [B, W], "bfloat16"),
    "q_sb": ("sbuf", [B, W], "bfloat16"),
    "msk": ("sbuf", [B, W], "bfloat16"),
    "b0": ("sbuf", [B, W], "bfloat16"),
    "b1": ("sbuf", [B, W], "bfloat16"),
    "s_sb": ("sbuf", [B, B], "bfloat16"),
    "relay": ("sbuf", [B, B], "bfloat16"),
    "y_sb": ("sbuf", [B, W], "bfloat16"),
    "s_ps": ("psum", [B, 512], "float32"),
    "a0_ps": ("psum", [B, 512], "float32"),
    "a1_ps": ("psum", [B, 512], "float32"),
    "y_ps": ("psum", [B, 512], "float32"),
}
for _r in range(N_RANKS - 1):
    SCRATCH["zin%d" % _r] = ("sbuf", [B, B], "bfloat16")

SEMAPHORES = ["ld_kv", "ld_kq", "ld_m", "fill", "s_mm", "s_cp", "a_mm", "b_rdy", "y_mm", "y_cp", "st",
              "sent", "h_in"] + ["a%d" % _r for _r in range(N_RANKS - 1)]


def _count(mask):
    return bin(mask).count("1")


def _plan(T, topo):
    cores = list(T.cores)
    n = len(cores)
    every = range(topo.CHIPS * topo.CORES_PER_CHIP)
    near, far = {}, {}
    for r, c in enumerate(cores):
        later = list(range(r + 1, n))
        near[r] = [d for d in later if topo.may_write(c, cores[d])]
        far[r] = []
        used = []
        for d in reversed(later):
            if topo.may_write(c, cores[d]):
                continue
            between = [s for s in range(r + 1, d) if not topo.may_write(cores[s], cores[d])]
            other_die = len(between) % 2 == 1
            spare = [x for x in every
                     if topo.chip(x) == topo.chip(c) and x not in cores and x not in used
                     and topo.may_write(x, cores[d])]
            spare.sort(key=lambda x: (topo.die(x) != topo.die(c)) != other_die)
            far[r].append((d, spare[0]))
            used.append(spare[0])
    return near, far


def _dst(topo, core):
    rid, pid, _ = topo.addr(core)
    return DstId(rid=rid, pnc=pid)


def _common_mask(topo, src, dsts):
    m = topo.mask(src, dsts[0])
    for d in dsts[1:]:
        m &= topo.mask(src, d)
    return m


def _relay_program(g, core, T, topo, r, d, far_r):
    src = T.cores[r]
    dst = T.cores[d]
    g.wait_ge(T.sem.h_in, _count(_common_mask(topo, src, [h for _, h in far_r])))
    rid, pid, _ = topo.addr(dst)
    mask = topo.mask(core, dst)
    g.remote_dma(out_ap=T["zin%d" % r][:], in_ap=T.relay[:], remote_sem=T.sem["a%d" % r], local_sem=T.sem.sent,
                 pid=pid, routing_id=rid, dma_engine_mask=mask)
    g.wait_ge(T.sem.sent, _count(mask))


def rank_program(g, core, T, topo):
    near, far = _plan(T, topo)
    cores = list(T.cores)
    n = len(cores)
    rank = T.rank_of(core)
    if rank is None:
        for r in range(n):
            for d, h in far[r]:
                if h == core:
                    _relay_program(g, core, T, topo, r, d, far[r])
        return

    sem = T.sem
    sends = rank < n - 1
    te, ve = g.tensor, g.vector

    n_kv = 16
    if sends:
        g.sync.dma_start(T.kt_sb[:], T.kt[:]).then_inc(sem.ld_kv, 16)
        n_kv = 32
    g.scalar.dma_start(T.v_sb[:], T.v[:]).then_inc(sem.ld_kv, 16)
    g.sync.dma_start(T.k_sb[:], T.k[:]).then_inc(sem.ld_kq, 16)
    g.scalar.dma_start(T.q_sb[:], T.q[:]).then_inc(sem.ld_kq, 16)
    g.sync.dma_start(T.msk[:, 0:B], T.m[:]).then_inc(sem.ld_m, 16)

    ve.memset(T.msk[:, B:W], 1.0).then_inc(sem.fill, 1)
    ve.memset(T.b1[:, 0:B], 0.0).then_inc(sem.fill, 1)

    te.wait_ge(sem.ld_kv, n_kv)
    if sends:
        te.matmul(T.s_ps[:, 0:B], T.kt_sb[:, 0:B], T.v_sb[:, 0:B], True, False)
        te.matmul(T.s_ps[:, 0:B], T.kt_sb[:, B:W], T.v_sb[:, B:W], False, True).then_inc(sem.s_mm, 1)
        ve.wait_ge(sem.s_mm, 1)
        ve.tensor_copy(T.s_sb[:], T.s_ps[:, 0:B]).then_inc(sem.s_cp, 1)

        g.wait_ge(sem.s_cp, 1)
        n_sent = 0
        if far[rank]:
            helpers = [h for _, h in far[rank]]
            mask = _common_mask(topo, core, helpers)
            g.remote_dma_fused([RemoteDMATransfer(
                dst_ids=[_dst(topo, h) for h in helpers], dma_engine_mask=mask, remote_sem=sem.h_in,
                srcs=[T.s_sb[:]], dsts=[T.relay[:] for _ in helpers], alu_op=0)], local_sem=sem.sent)
            n_sent += _count(mask)
        if near[rank]:
            dsts = [cores[d] for d in near[rank]]
            mask = _common_mask(topo, core, dsts)
            g.remote_dma_fused([RemoteDMATransfer(
                dst_ids=[_dst(topo, c) for c in dsts], dma_engine_mask=mask, remote_sem=sem["a%d" % rank],
                srcs=[T.s_sb[:]], dsts=[T["zin%d" % rank][:] for _ in dsts], alu_op=0)], local_sem=sem.sent)
            n_sent += _count(mask)
        g.wait_ge(sem.sent, n_sent)

    te.wait_ge(sem.ld_kq, 32)
    te.matmul(T.a0_ps[:, 0:W], T.k_sb[:, 0:B], T.q_sb[:, 0:W], True, True).then_inc(sem.a_mm, 1)
    te.matmul(T.a1_ps[:, 0:B], T.k_sb[:, B:W], T.q_sb[:, B:W], True, True).then_inc(sem.a_mm, 1)
    ve.wait_ge(sem.a_mm, 2)
    ve.wait_ge(sem.ld_m, 16)
    ve.wait_ge(sem.fill, 2)
    ve.tensor_tensor(T.b0[:, 0:W], T.a0_ps[:, 0:W], T.msk[:, 0:W], AluOpType.mult).then_inc(sem.b_rdy, 1)
    ve.tensor_tensor(T.b1[:, B:W], T.a1_ps[:, 0:B], T.msk[:, 0:B], AluOpType.mult).then_inc(sem.b_rdy, 1)

    arrivals = []
    for s in range(rank):
        if rank in near[s]:
            arrivals.append((s, _count(_common_mask(topo, cores[s], [cores[d] for d in near[s]]))))
    for s in reversed(range(rank)):
        for d, h in far[s]:
            if d == rank:
                arrivals.append((s, _count(topo.mask(h, core))))
    te.wait_ge(sem.b_rdy, 2)
    te.wait_ge(sem.fill, 2)
    te.matmul(T.y_ps[:, 0:W], T.v_sb[:, 0:B], T.b0[:, 0:W], True, False)
    last = te.matmul(T.y_ps[:, 0:W], T.v_sb[:, B:W], T.b1[:, 0:W], False, not arrivals)
    for i, (s, inc) in enumerate(arrivals):
        te.wait_ge(sem["a%d" % s], inc)
        last = te.matmul(T.y_ps[:, 0:W], T["zin%d" % s][:], T.q_sb[:, 0:W], False, i == len(arrivals) - 1)
    last.then_inc(sem.y_mm, 1)

    ve.wait_ge(sem.y_mm, 1)
    ve.tensor_copy(T.y_sb[:], T.y_ps[:, 0:W]).then_inc(sem.y_cp, 1)
    g.sync.wait_ge(sem.y_cp, 1)
    g.sync.dma_start(T.y[:], T.y_sb[:]).then_inc(sem.st, 16)
    g.sync.wait_ge(sem.st, 16)
